import numpy as np, ml_dtypes
CORES = [4,20,60,84,92,100,116]
N = 7
R, T = 4096, 512
def entries(a): return a.T.reshape(-1)
def pack(v, P): return np.ascontiguousarray(np.asarray(v, np.int32).reshape(-1, P).T)
def lists(rng, how):
    I = rng.integers(0, N * R, (N, T))
    if how == "alike": I[:] = rng.integers(0, N * R, (N, 1))
    if how == "distinct": I = np.stack([rng.permutation(N * R)[:T] for r in range(N)])
    if how == "hotrank": I = R * int(rng.integers(N)) + rng.integers(0, R, (N, T))
    if how == "own": I = R * np.arange(N).reshape(N, 1) + rng.integers(0, R, (N, T))
    if how == "edge": I = R * rng.integers(0, N, (N, T)) + np.where(rng.random((N, T)) < 0.5, 0, R - 1)
    return {"idx": np.stack([pack(I[r], 16) for r in range(N)])}
def setup_inputs(rng):
    return dict({"x": rng.standard_normal((N, 128, T), dtype=np.float32).astype(ml_dtypes.bfloat16), "tab": rng.standard_normal((N, 128, R), dtype=np.float32).astype(ml_dtypes.bfloat16)}, **lists(rng, "uniform"))
def setup_inputs_alike(rng):
    d = setup_inputs(rng); d.update(lists(rng, "alike"))
    for k in ("x", "tab"): d[k] = (d[k].astype(np.float32) * 1024.0).astype(d[k].dtype)
    return d
def setup_inputs_distinct(rng):
    d = setup_inputs(rng); d.update(lists(rng, "distinct"))
    for k in ("x", "tab"): d[k] = (d[k].astype(np.float32) * (1 / 1024.0)).astype(d[k].dtype)
    return d
def setup_inputs_edge(rng):
    d = setup_inputs(rng); d.update(lists(rng, "edge"))
    return d
def setup_inputs_hotrank(rng):
    d = setup_inputs(rng); d.update(lists(rng, "hotrank"))
    return d
def setup_inputs_own(rng):
    d = setup_inputs(rng); d.update(lists(rng, "own"))
    return d
def check_inputs(x):
    bad = []
    if x["idx"].min() < 0 or x["idx"].max() >= N * R: bad.append("idx out of range")
    return bad
def reference(x, tab, idx):
    A = np.concatenate(list(tab), axis=1).astype(np.float64)
    return {"y": np.stack([x[r].astype(np.float64) + A[:, entries(idx[r])] for r in range(N)]).astype(ml_dtypes.bfloat16)}

@@ -1,0 +1,207 @@
+from concourse.bass import DstId, RemoteDMATransfer
+from concourse.mybir import AluOpType, ActivationFunctionType
+
+N = 7
+PART = 4096
+COLS = 512
+K = 32
+PAD = 8
+WIN = PART + 2 * PAD
+
+SCRATCH = {
+    "rep": ("dram", [128, K], "int32"),
+    "lists": ("sbuf", [128, N * K], "int32"),
+    "off": ("sbuf", [128, N * K], "uint16"),
+    "win": ("sbuf", [128, WIN], "bfloat16"),
+    "xs": ("sbuf", [128, COLS], "bfloat16"),
+    "ident": ("sbuf", [128, 128], "bfloat16"),
+    "blk": ("sbuf", [128, N * COLS], "bfloat16"),
+    "land": ("sbuf", [128, N * COLS], "bfloat16"),
+    "rly": ("sbuf", [128, (N - 1) * COLS], "bfloat16"),
+    "res": ("sbuf", [128, COLS], "bfloat16"),
+    "acc": ("psum", [128, COLS], "float32"),
+}
+SEMAPHORES = (["rep", "ownl", "tabl", "xl", "pad", "one", "idn", "lst", "snt", "pe", "cp", "st"]
+              + ["l%d" % i for i in range(N)] + ["o%d" % i for i in range(N)]
+              + ["g%d" % i for i in range(N)] + ["d%d" % i for i in range(N)]
+              + ["h%d" % i for i in range(N - 1)])
+
+
+def _bits(m):
+    return bin(m).count("1")
+
+
+def _plan(T, topo):
+    cores = list(T.cores)
+    n = len(cores)
+    every = range(topo.CORES_PER_CHIP * topo.CHIPS)
+    cls = [[j for j in range(n) if j == s or topo.may_write(cores[s], cores[j])] for s in range(n)]
+    k = [cls[s].index(s) for s in range(n)]
+    near_out, near_in, far, relay, tasks = [], [], [], [], {}
+    for s in range(n):
+        m = len(cls[s])
+        near_out.append([cls[s][(k[s] + 1 + i) % m] for i in range(m - 1)])
+        near_in.append([cls[s][(k[s] - 1 - i) % m] for i in range(m - 1)])
+        raw = [j for j in range(n) if j not in cls[s]]
+        far.append([raw[(i + k[s]) % len(raw)] for i in range(len(raw))])
+    for s in range(n):
+        me = cores[s]
+        own = [c for c in every if topo.chip(c) == topo.chip(me) and c not in cores
+               and all(topo.may_write(c, cores[j]) for j in far[s])]
+        dies = [[c for c in own if topo.die(c) == topo.die(me)], [c for c in own if topo.die(c) != topo.die(me)]]
+        cnt = [0, 0]
+        via = {}
+        for r in far[s]:
+            d = (k[s] + k[r]) % 2
+            if not dies[d]:
+                d = 1 - d
+            h = dies[d][cnt[d] % len(dies[d])]
+            cnt[d] += 1
+            via[r] = h
+            tasks.setdefault(h, (s, []))[1].append(r)
+        relay.append(via)
+    return cores, near_out, near_in, far, relay, tasks
+
+
+def _send(g, T, topo, src, dsts, aps, sem, mask):
+    ids = []
+    for c in dsts:
+        rid, pid, _ = topo.addr(c)
+        ids.append(DstId(rid=rid, pnc=pid))
+    g.remote_dma_fused([RemoteDMATransfer(dst_ids=ids, dma_engine_mask=mask, remote_sem=sem,
+                                          srcs=[src], dsts=aps, alu_op=0)], local_sem=T.sem.snt)
+    return _bits(mask)
+
+
+def _helper(g, core, T, topo, cores, job, relay):
+    s, dst = job
+    me = cores[s]
+    sent = 0
+    hi = _chip_only(topo, me, cores, relay[s])
+    g.wait_ge(T.sem.lst, _bits(hi))
+    mask = topo.mask(core, cores[dst[0]])
+    for r in dst:
+        mask &= topo.mask(core, cores[r])
+    sent += _send(g, T, topo, T.rep[:, :], [cores[r] for r in dst],
+                  [T.lists[:, s * K:(s + 1) * K] for r in dst], T.sem["l%d" % s], mask)
+    for i, r in enumerate(dst):
+        g.wait_ge(T.sem["h%d" % i], _bits(_block_mask(topo, me, cores, relay[s], s)))
+        sent += _send(g, T, topo, T.rly[:, i * COLS:(i + 1) * COLS], [cores[r]],
+                      [T.land[:, s * COLS:(s + 1) * COLS]], T.sem["d%d" % s], topo.mask(core, cores[r]))
+    g.wait_ge(T.sem.snt, sent)
+
+
+def _chip_only(topo, me, cores, via):
+    on = 0
+    for h in via.values():
+        on = topo.mask(me, h) if not on else on & topo.mask(me, h)
+    out = 0
+    for c in cores:
+        if c != me and topo.chip(c) != topo.chip(me):
+            out |= topo.mask(me, c)
+    return (on & ~out) or on
+
+
+def _block_mask(topo, me, cores, via, s):
+    near = [c for c in cores if c != me and topo.may_write(me, c)]
+    if len(near) > 1:
+        return _chip_only(topo, me, cores, via)
+    on = 0
+    for h in via.values():
+        on = topo.mask(me, h) if not on else on & topo.mask(me, h)
+    return on
+
+
+def rank_program(g, core, T, topo):
+    cores, near_out, near_in, far, relay, tasks = _plan(T, topo)
+    rank = T.rank_of(core)
+    if rank is None:
+        if core in tasks:
+            _helper(g, core, T, topo, cores, tasks[core], relay)
+        return
+    s = rank
+    sem = T.sem
+    v, a, pe, sy = g.vector, g.scalar, g.tensor, g.sync
+
+    for q in range(8):
+        (sy if q % 2 == 0 else a).dma_start(T.rep[16 * q:16 * q + 16, :], T.idx[:, :]).then_inc(sem.rep, 16)
+    sy.dma_start(T.win[:, PAD:PAD + PART], T.tab[:, :]).then_inc(sem.tabl, 16)
+    a.dma_start(T.xs[:, :], T.x[:, :]).then_inc(sem.xl, 16)
+    a.wait_ge(sem.rep, 128)
+    a.dma_start(T.lists[:, s * K:(s + 1) * K], T.rep[:, :]).then_inc(sem.ownl, 16)
+
+    v.memset(T.ident[:, :], 1.0).then_inc(sem.one, 1)
+    v.memset(T.win[:, 0:PAD], 0.0).then_inc(sem.pad, 1)
+    v.memset(T.win[:, PAD + PART:WIN], 0.0).then_inc(sem.pad, 1)
+    g.wait_ge(sem.one, 1)
+    g.affine_select(T.ident[:, :], T.ident[:, :], [[-1, 128]], AluOpType.is_equal, 0.0, 0, 1).then_inc(sem.idn, 1)
+
+    sent = 0
+    hi = _chip_only(topo, core, cores, relay[s])
+    helpers = []
+    for r in far[s]:
+        if relay[s][r] not in helpers:
+            helpers.append(relay[s][r])
+    g.wait_ge(sem.rep, 128)
+    if helpers:
+        sent += _send(g, T, topo, T.rep[:, :], helpers, [T.rep[:, :] for h in helpers], sem.lst, hi)
+    if near_out[s]:
+        mask = topo.mask(core, cores[near_out[s][0]])
+        for r in near_out[s]:
+            mask &= topo.mask(core, cores[r])
+        sent += _send(g, T, topo, T.rep[:, :], [cores[r] for r in near_out[s]],
+                      [T.lists[:, s * K:(s + 1) * K] for r in near_out[s]], sem["l%d" % s], mask)
+
+    v.wait_ge(sem.pad, 2)
+    v.wait_ge(sem.tabl, 16)
+    a.wait_ge(sem.pad, 2)
+    a.wait_ge(sem.tabl, 16)
+    half = K // 2
+    for r in [s] + near_in[s] + far[s]:
+        if r == s:
+            v.wait_ge(sem.ownl, 16)
+        elif r in near_in[s]:
+            v.wait_ge(sem["l%d" % r], _bits(topo.mask(cores[r], core)))
+        else:
+            v.wait_ge(sem["l%d" % r], _bits(topo.mask(relay[r][s], core)))
+        v.tensor_scalar(T.off[:, r * K:(r + 1) * K], T.lists[:, r * K:(r + 1) * K], PAD - PART * s, PAD + PART,
+                        AluOpType.add, AluOpType.min).then_inc(sem["o%d" % r], 1)
+        v.wait_ge(sem["o%d" % r], 1)
+        a.wait_ge(sem["o%d" % r], 1)
+        a.activation(T.blk[:, r * COLS:r * COLS + COLS // 2],
+                     T.win[:, 0:WIN].indirect(T.off[:, r * K:r * K + half]),
+                     ActivationFunctionType.Copy).then_inc(sem["g%d" % r], 1)
+        v.tensor_copy(T.blk[:, r * COLS + COLS // 2:(r + 1) * COLS],
+                      T.win[:, 0:WIN].indirect(T.off[:, r * K + half:(r + 1) * K])).then_inc(sem["g%d" % r], 1)
+
+    bm = _block_mask(topo, core, cores, relay[s], s) if far[s] else 0
+    for r in near_in[s]:
+        g.wait_ge(sem["g%d" % r], 2)
+        sent += _send(g, T, topo, T.blk[:, r * COLS:(r + 1) * COLS], [cores[r]],
+                      [T.land[:, s * COLS:(s + 1) * COLS]], sem["d%d" % s], topo.mask(core, cores[r]))
+    for r in far[s]:
+        h = relay[s][r]
+        i = tasks[h][1].index(r)
+        g.wait_ge(sem["g%d" % r], 2)
+        sent += _send(g, T, topo, T.blk[:, r * COLS:(r + 1) * COLS], [h],
+                      [T.rly[:, i * COLS:(i + 1) * COLS]], sem["h%d" % i], bm)
+
+    pe.wait_ge(sem.idn, 1)
+    pe.wait_ge(sem.xl, 16)
+    pe.matmul(T.acc[:, :], T.ident[:, :], T.xs[:, :], True, False)
+    pe.wait_ge(sem["g%d" % s], 2)
+    pe.matmul(T.acc[:, :], T.ident[:, :], T.blk[:, s * COLS:(s + 1) * COLS], False, False)
+    late = sorted(far[s], key=lambda o: far[o].index(s))
+    order = near_out[s] + late
+    for n_, o in enumerate(order):
+        last_hop = cores[o] if o in near_out[s] else relay[o][s]
+        pe.wait_ge(sem["d%d" % o], _bits(topo.mask(last_hop, core)))
+        mm = pe.matmul(T.acc[:, :], T.ident[:, :], T.land[:, o * COLS:(o + 1) * COLS], False, n_ == len(order) - 1)
+        if n_ == len(order) - 1:
+            mm.then_inc(sem.pe, 1)
+    v.wait_ge(sem.pe, 1)
+    v.tensor_copy(T.res[:, :], T.acc[:, :]).then_inc(sem.cp, 1)
+    sy.wait_ge(sem.cp, 1)
+    sy.dma_start(T.y[:, :], T.res[:, :]).then_inc(sem.st, 16)
+    sy.wait_ge(sem.st, 16)
+    g.wait_ge(sem.snt, sent)

@@ -5,6 +5,8 @@ N = 7
 PART = 4096
 COLS = 512
 K = 32
+KS = 18
+SP = 16 * KS
 PAD = 8
 WIN = PART + 2 * PAD
 
@@ -23,8 +25,8 @@ SCRATCH = {
 }
 SEMAPHORES = (["rep", "ownl", "tabl", "xl", "pad", "one", "idn", "lst", "snt", "pe", "cp", "st"]
               + ["l%d" % i for i in range(N)] + ["o%d" % i for i in range(N)]
-              + ["g%d" % i for i in range(N)] + ["d%d" % i for i in range(N)]
-              + ["h%d" % i for i in range(N - 1)])
+              + ["gs%d" % i for i in range(N)] + ["gv%d" % i for i in range(N)]
+              + ["d%d" % i for i in range(N)] + ["h%d" % i for i in range(N - 1)])
 
 
 def _bits(m):
@@ -37,7 +39,7 @@ def _plan(T, topo):
     every = range(topo.CORES_PER_CHIP * topo.CHIPS)
     cls = [[j for j in range(n) if j == s or topo.may_write(cores[s], cores[j])] for s in range(n)]
     k = [cls[s].index(s) for s in range(n)]
-    near_out, near_in, far, relay, tasks = [], [], [], [], {}
+    near_out, near_in, far, fwd, route, tasks, lmask = [], [], [], [], [], {}, []
     for s in range(n):
         m = len(cls[s])
         near_out.append([cls[s][(k[s] + 1 + i) % m] for i in range(m - 1)])
@@ -46,21 +48,50 @@ def _plan(T, topo):
         far.append([raw[(i + k[s]) % len(raw)] for i in range(len(raw))])
     for s in range(n):
         me = cores[s]
-        own = [c for c in every if topo.chip(c) == topo.chip(me) and c not in cores
-               and all(topo.may_write(c, cores[j]) for j in far[s])]
+        mine = [c for c in every if topo.chip(c) == topo.chip(me) and c not in cores]
+        own = [c for c in mine if all(topo.may_write(c, cores[j]) for j in far[s])]
         dies = [[c for c in own if topo.die(c) == topo.die(me)], [c for c in own if topo.die(c) != topo.die(me)]]
+        on = topo.mask(me, mine[0])
+        out = 0
+        for c in cores:
+            if topo.chip(c) != topo.chip(me):
+                out |= topo.mask(me, c)
+        hi = (on & ~out) or on
+        lmask.append(hi)
+        many = len(near_in[s]) > 1
         cnt = [0, 0]
-        via = {}
+        f, w = {}, {}
+
+        def put(h, r, c0, c1, mask):
+            t = tasks.setdefault(h, (s, [], []))
+            t[2].append((r, c0, c1, _bits(mask)))
+            w.setdefault(r, []).append((h, len(t[2]) - 1, c0, c1, mask))
+
         for r in far[s]:
             d = (k[s] + k[r]) % 2
-            if not dies[d]:
-                d = 1 - d
-            h = dies[d][cnt[d] % len(dies[d])]
+            hs = [dies[d][cnt[d]]] if cnt[d] < len(dies[d]) else dies[d][:2]
             cnt[d] += 1
-            via[r] = h
-            tasks.setdefault(h, (s, []))[1].append(r)
-        relay.append(via)
-    return cores, near_out, near_in, far, relay, tasks
+            f[r] = hs[0]
+            tasks.setdefault(hs[0], (s, [], []))[1].append(r)
+            mask = hi if many else on
+            if len(hs) == 1:
+                put(hs[0], r, 0, COLS, mask)
+            else:
+                put(hs[0], r, 0, SP, mask)
+                put(hs[1], r, SP, COLS, mask)
+        idle = [c for c in mine if c not in tasks and topo.die(c) != topo.die(me)]
+        if len(near_in[s]) >= 4:
+            for r in near_in[s][:len(near_in[s]) // 2]:
+                fit = [c for c in idle if topo.may_write(c, cores[r])]
+                if fit:
+                    idle.remove(fit[0])
+                    put(fit[0], r, 0, COLS, hi)
+        fwd.append(f)
+        route.append(w)
+    for s in range(n):
+        if all(len(tasks[p[0]][2]) == 1 for r in far[s] for p in route[s][r]):
+            far[s] = sorted(far[s], key=lambda r: tasks[fwd[r][s]][1].index(s))
+    return cores, near_out, near_in, far, fwd, route, tasks, lmask
 
 
 def _send(g, T, topo, src, dsts, aps, sem, mask):
@@ -73,51 +104,34 @@ def _send(g, T, topo, src, dsts, aps, sem, mask):
     return _bits(mask)
 
 
-def _helper(g, core, T, topo, cores, job, relay):
-    s, dst = job
-    me = cores[s]
+def _common(topo, me, dsts):
+    m = topo.mask(me, dsts[0])
+    for c in dsts:
+        m &= topo.mask(me, c)
+    return m
+
+
+def _helper(g, core, T, topo, cores, job, lmask):
+    s, pas, pieces = job
     sent = 0
-    hi = _chip_only(topo, me, cores, relay[s])
-    g.wait_ge(T.sem.lst, _bits(hi))
-    mask = topo.mask(core, cores[dst[0]])
-    for r in dst:
-        mask &= topo.mask(core, cores[r])
-    sent += _send(g, T, topo, T.rep[:, :], [cores[r] for r in dst],
-                  [T.lists[:, s * K:(s + 1) * K] for r in dst], T.sem["l%d" % s], mask)
-    for i, r in enumerate(dst):
-        g.wait_ge(T.sem["h%d" % i], _bits(_block_mask(topo, me, cores, relay[s], s)))
-        sent += _send(g, T, topo, T.rly[:, i * COLS:(i + 1) * COLS], [cores[r]],
-                      [T.land[:, s * COLS:(s + 1) * COLS]], T.sem["d%d" % s], topo.mask(core, cores[r]))
+    if pas:
+        g.wait_ge(T.sem.lst, _bits(lmask[s]))
+        to = [cores[r] for r in pas]
+        sent += _send(g, T, topo, T.rep[:, :], to, [T.lists[:, s * K:(s + 1) * K] for c in to],
+                      T.sem["l%d" % s], _common(topo, core, to))
+    for i, (r, c0, c1, cnt) in enumerate(pieces):
+        g.wait_ge(T.sem["h%d" % i], cnt)
+        sent += _send(g, T, topo, T.rly[:, i * COLS:i * COLS + c1 - c0], [cores[r]],
+                      [T.land[:, s * COLS + c0:s * COLS + c1]], T.sem["d%d" % s], topo.mask(core, cores[r]))
     g.wait_ge(T.sem.snt, sent)
 
 
-def _chip_only(topo, me, cores, via):
-    on = 0
-    for h in via.values():
-        on = topo.mask(me, h) if not on else on & topo.mask(me, h)
-    out = 0
-    for c in cores:
-        if c != me and topo.chip(c) != topo.chip(me):
-            out |= topo.mask(me, c)
-    return (on & ~out) or on
-
-
-def _block_mask(topo, me, cores, via, s):
-    near = [c for c in cores if c != me and topo.may_write(me, c)]
-    if len(near) > 1:
-        return _chip_only(topo, me, cores, via)
-    on = 0
-    for h in via.values():
-        on = topo.mask(me, h) if not on else on & topo.mask(me, h)
-    return on
-
-
 def rank_program(g, core, T, topo):
-    cores, near_out, near_in, far, relay, tasks = _plan(T, topo)
+    cores, near_out, near_in, far, fwd, route, tasks, lmask = _plan(T, topo)
     rank = T.rank_of(core)
     if rank is None:
         if core in tasks:
-            _helper(g, core, T, topo, cores, tasks[core], relay)
+            _helper(g, core, T, topo, cores, tasks[core], lmask)
         return
     s = rank
     sem = T.sem
@@ -137,70 +151,95 @@ def rank_program(g, core, T, topo):
     g.affine_select(T.ident[:, :], T.ident[:, :], [[-1, 128]], AluOpType.is_equal, 0.0, 0, 1).then_inc(sem.idn, 1)
 
     sent = 0
-    hi = _chip_only(topo, core, cores, relay[s])
     helpers = []
     for r in far[s]:
-        if relay[s][r] not in helpers:
-            helpers.append(relay[s][r])
+        if fwd[s][r] not in helpers:
+            helpers.append(fwd[s][r])
     g.wait_ge(sem.rep, 128)
-    if helpers:
-        sent += _send(g, T, topo, T.rep[:, :], helpers, [T.rep[:, :] for h in helpers], sem.lst, hi)
-    if near_out[s]:
-        mask = topo.mask(core, cores[near_out[s][0]])
-        for r in near_out[s]:
-            mask &= topo.mask(core, cores[r])
-        sent += _send(g, T, topo, T.rep[:, :], [cores[r] for r in near_out[s]],
-                      [T.lists[:, s * K:(s + 1) * K] for r in near_out[s]], sem["l%d" % s], mask)
+    sent += _send(g, T, topo, T.rep[:, :], helpers, [T.rep[:, :] for h in helpers], sem.lst, lmask[s])
+    to = [cores[r] for r in near_out[s]]
+    sent += _send(g, T, topo, T.rep[:, :], to, [T.lists[:, s * K:(s + 1) * K] for c in to], sem["l%d" % s],
+                  _common(topo, core, to))
 
-    v.wait_ge(sem.pad, 2)
-    v.wait_ge(sem.tabl, 16)
-    a.wait_ge(sem.pad, 2)
-    a.wait_ge(sem.tabl, 16)
-    half = K // 2
-    for r in [s] + near_in[s] + far[s]:
+    for q in (v, a):
+        q.wait_ge(sem.pad, 2)
+        q.wait_ge(sem.tabl, 16)
+
+    def offsets(r):
         if r == s:
             v.wait_ge(sem.ownl, 16)
-        elif r in near_in[s]:
-            v.wait_ge(sem["l%d" % r], _bits(topo.mask(cores[r], core)))
         else:
-            v.wait_ge(sem["l%d" % r], _bits(topo.mask(relay[r][s], core)))
+            v.wait_ge(sem["l%d" % r], _bits(topo.mask(fwd[r][s] if s in fwd[r] else cores[r], core)))
         v.tensor_scalar(T.off[:, r * K:(r + 1) * K], T.lists[:, r * K:(r + 1) * K], PAD - PART * s, PAD + PART,
                         AluOpType.add, AluOpType.min).then_inc(sem["o%d" % r], 1)
+
+    def gather(r):
         v.wait_ge(sem["o%d" % r], 1)
         a.wait_ge(sem["o%d" % r], 1)
-        a.activation(T.blk[:, r * COLS:r * COLS + COLS // 2],
-                     T.win[:, 0:WIN].indirect(T.off[:, r * K:r * K + half]),
-                     ActivationFunctionType.Copy).then_inc(sem["g%d" % r], 1)
-        v.tensor_copy(T.blk[:, r * COLS + COLS // 2:(r + 1) * COLS],
-                      T.win[:, 0:WIN].indirect(T.off[:, r * K + half:(r + 1) * K])).then_inc(sem["g%d" % r], 1)
+        a.activation(T.blk[:, r * COLS:r * COLS + SP], T.win[:, 0:WIN].indirect(T.off[:, r * K:r * K + KS]),
+                     ActivationFunctionType.Copy).then_inc(sem["gs%d" % r], 1)
+        v.tensor_copy(T.blk[:, r * COLS + SP:(r + 1) * COLS],
+                      T.win[:, 0:WIN].indirect(T.off[:, r * K + KS:(r + 1) * K])).then_inc(sem["gv%d" % r], 1)
 
-    bm = _block_mask(topo, core, cores, relay[s], s) if far[s] else 0
-    for r in near_in[s]:
-        g.wait_ge(sem["g%d" % r], 2)
-        sent += _send(g, T, topo, T.blk[:, r * COLS:(r + 1) * COLS], [cores[r]],
-                      [T.land[:, s * COLS:(s + 1) * COLS]], sem["d%d" % s], topo.mask(core, cores[r]))
-    for r in far[s]:
-        h = relay[s][r]
-        i = tasks[h][1].index(r)
-        g.wait_ge(sem["g%d" % r], 2)
-        sent += _send(g, T, topo, T.blk[:, r * COLS:(r + 1) * COLS], [h],
-                      [T.rly[:, i * COLS:(i + 1) * COLS]], sem["h%d" % i], bm)
+    hold = 1 if len(near_in[s]) >= 4 else 0
+    first = near_in[s][:len(near_in[s]) - hold]
+    last = near_in[s][len(near_in[s]) - hold:]
+    ahead = len(far[s]) > 2
+    for r in [s] + first:
+        offsets(r)
+        gather(r)
+    if ahead:
+        offsets(far[s][0])
+    for i, r in enumerate(far[s]):
+        if not ahead:
+            offsets(r)
+        elif i + 1 < len(far[s]):
+            offsets(far[s][i + 1])
+        gather(r)
+    for r in last:
+        offsets(r)
+        gather(r)
+
+    for r in first + far[s] + last:
+        if r in route[s]:
+            for h, i, c0, c1, mask in route[s][r]:
+                if c0 < SP:
+                    g.wait_ge(sem["gs%d" % r], 1)
+                if c1 > SP:
+                    g.wait_ge(sem["gv%d" % r], 1)
+                sent += _send(g, T, topo, T.blk[:, r * COLS + c0:r * COLS + c1], [h],
+                              [T.rly[:, i * COLS:i * COLS + c1 - c0]], sem["h%d" % i], mask)
+        else:
+            g.wait_ge(sem["gs%d" % r], 1)
+            g.wait_ge(sem["gv%d" % r], 1)
+            sent += _send(g, T, topo, T.blk[:, r * COLS:(r + 1) * COLS], [cores[r]],
+                          [T.land[:, s * COLS:(s + 1) * COLS]], sem["d%d" % s], topo.mask(core, cores[r]))
 
     pe.wait_ge(sem.idn, 1)
     pe.wait_ge(sem.xl, 16)
     pe.matmul(T.acc[:, :], T.ident[:, :], T.xs[:, :], True, False)
-    pe.wait_ge(sem["g%d" % s], 2)
+    pe.wait_ge(sem["gs%d" % s], 1)
+    pe.wait_ge(sem["gv%d" % s], 1)
     pe.matmul(T.acc[:, :], T.ident[:, :], T.blk[:, s * COLS:(s + 1) * COLS], False, False)
+    straight = [o for o in near_out[s] if s not in route[o]]
+    passed = [o for o in near_out[s] if s in route[o]]
     late = sorted(far[s], key=lambda o: far[o].index(s))
-    order = near_out[s] + late
-    for n_, o in enumerate(order):
-        last_hop = cores[o] if o in near_out[s] else relay[o][s]
-        pe.wait_ge(sem["d%d" % o], _bits(topo.mask(last_hop, core)))
-        mm = pe.matmul(T.acc[:, :], T.ident[:, :], T.land[:, o * COLS:(o + 1) * COLS], False, n_ == len(order) - 1)
-        if n_ == len(order) - 1:
+    order = straight[:len(straight) - hold] + passed + straight[len(straight) - hold:] + late
+
+    def landed(o):
+        if s in route[o]:
+            return sum(_bits(topo.mask(p[0], core)) for p in route[o][s])
+        return _bits(topo.mask(cores[o], core))
+
+    for n_, o in enumerate(order[:-1]):
+        pe.wait_ge(sem["d%d" % o], landed(o))
+        mm = pe.matmul(T.acc[:, :], T.ident[:, :], T.land[:, o * COLS:(o + 1) * COLS], False, n_ == len(order) - 2)
+        if n_ == len(order) - 2:
             mm.then_inc(sem.pe, 1)
+    o = order[-1]
     v.wait_ge(sem.pe, 1)
-    v.tensor_copy(T.res[:, :], T.acc[:, :]).then_inc(sem.cp, 1)
+    v.wait_ge(sem["d%d" % o], landed(o))
+    v.tensor_tensor(T.res[:, :], T.acc[:, :], T.land[:, o * COLS:(o + 1) * COLS], AluOpType.add).then_inc(sem.cp, 1)
     sy.wait_ge(sem.cp, 1)
     sy.dma_start(T.y[:, :], T.res[:, :]).then_inc(sem.st, 16)
     sy.wait_ge(sem.st, 16)

from concourse.bass import DstId, RemoteDMATransfer
from concourse.mybir import AluOpType, ActivationFunctionType

N = 7
PART = 4096
COLS = 512
K = 32
KS = 18
SP = 16 * KS
PAD = 8
WIN = PART + 2 * PAD

SCRATCH = {
    "rep": ("dram", [128, K], "int32"),
    "lists": ("sbuf", [128, N * K], "int32"),
    "off": ("sbuf", [128, N * K], "uint16"),
    "win": ("sbuf", [128, WIN], "bfloat16"),
    "xs": ("sbuf", [128, COLS], "bfloat16"),
    "ident": ("sbuf", [128, 128], "bfloat16"),
    "blk": ("sbuf", [128, N * COLS], "bfloat16"),
    "land": ("sbuf", [128, N * COLS], "bfloat16"),
    "rly": ("sbuf", [128, (N - 1) * COLS], "bfloat16"),
    "res": ("sbuf", [128, COLS], "bfloat16"),
    "acc": ("psum", [128, COLS], "float32"),
}
SEMAPHORES = (["rep", "ownl", "tabl", "xl", "pad", "one", "idn", "lst", "snt", "pe", "cp", "st"]
              + ["l%d" % i for i in range(N)] + ["o%d" % i for i in range(N)]
              + ["gs%d" % i for i in range(N)] + ["gv%d" % i for i in range(N)]
              + ["d%d" % i for i in range(N)] + ["h%d" % i for i in range(N - 1)])


def _bits(m):
    return bin(m).count("1")


def _plan(T, topo):
    cores = list(T.cores)
    n = len(cores)
    every = range(topo.CORES_PER_CHIP * topo.CHIPS)
    cls = [[j for j in range(n) if j == s or topo.may_write(cores[s], cores[j])] for s in range(n)]
    k = [cls[s].index(s) for s in range(n)]
    near_out, near_in, far, fwd, route, tasks, lmask = [], [], [], [], [], {}, []
    for s in range(n):
        m = len(cls[s])
        near_out.append([cls[s][(k[s] + 1 + i) % m] for i in range(m - 1)])
        near_in.append([cls[s][(k[s] - 1 - i) % m] for i in range(m - 1)])
        raw = [j for j in range(n) if j not in cls[s]]
        far.append([raw[(i + k[s]) % len(raw)] for i in range(len(raw))])
    for s in range(n):
        me = cores[s]
        mine = [c for c in every if topo.chip(c) == topo.chip(me) and c not in cores]
        own = [c for c in mine if all(topo.may_write(c, cores[j]) for j in far[s])]
        dies = [[c for c in own if topo.die(c) == topo.die(me)], [c for c in own if topo.die(c) != topo.die(me)]]
        on = topo.mask(me, mine[0])
        out = 0
        for c in cores:
            if topo.chip(c) != topo.chip(me):
                out |= topo.mask(me, c)
        hi = (on & ~out) or on
        lmask.append(hi)
        many = len(near_in[s]) > 1
        cnt = [0, 0]
        f, w = {}, {}

        def put(h, r, c0, c1, mask):
            t = tasks.setdefault(h, (s, [], []))
            t[2].append((r, c0, c1, _bits(mask)))
            w.setdefault(r, []).append((h, len(t[2]) - 1, c0, c1, mask))

        for r in far[s]:
            d = (k[s] + k[r]) % 2
            hs = [dies[d][cnt[d]]] if cnt[d] < len(dies[d]) else dies[d][:2]
            cnt[d] += 1
            f[r] = hs[0]
            tasks.setdefault(hs[0], (s, [], []))[1].append(r)
            mask = hi if many else on
            if len(hs) == 1:
                put(hs[0], r, 0, COLS, mask)
            else:
                put(hs[0], r, 0, SP, mask)
                put(hs[1], r, SP, COLS, mask)
        idle = [c for c in mine if c not in tasks and topo.die(c) != topo.die(me)]
        if len(near_in[s]) >= 4:
            for r in near_in[s][:len(near_in[s]) // 2]:
                fit = [c for c in idle if topo.may_write(c, cores[r])]
                if fit:
                    idle.remove(fit[0])
                    put(fit[0], r, 0, COLS, hi)
        fwd.append(f)
        route.append(w)
    for s in range(n):
        if all(len(tasks[p[0]][2]) == 1 for r in far[s] for p in route[s][r]):
            far[s] = sorted(far[s], key=lambda r: tasks[fwd[r][s]][1].index(s))
    return cores, near_out, near_in, far, fwd, route, tasks, lmask


def _send(g, T, topo, src, dsts, aps, sem, mask):
    ids = []
    for c in dsts:
        rid, pid, _ = topo.addr(c)
        ids.append(DstId(rid=rid, pnc=pid))
    g.remote_dma_fused([RemoteDMATransfer(dst_ids=ids, dma_engine_mask=mask, remote_sem=sem,
                                          srcs=[src], dsts=aps, alu_op=0)], local_sem=T.sem.snt)
    return _bits(mask)


def _common(topo, me, dsts):
    m = topo.mask(me, dsts[0])
    for c in dsts:
        m &= topo.mask(me, c)
    return m


def _helper(g, core, T, topo, cores, job, lmask):
    s, pas, pieces = job
    sent = 0
    if pas:
        g.wait_ge(T.sem.lst, _bits(lmask[s]))
        to = [cores[r] for r in pas]
        sent += _send(g, T, topo, T.rep[:, :], to, [T.lists[:, s * K:(s + 1) * K] for c in to],
                      T.sem["l%d" % s], _common(topo, core, to))
    for i, (r, c0, c1, cnt) in enumerate(pieces):
        g.wait_ge(T.sem["h%d" % i], cnt)
        sent += _send(g, T, topo, T.rly[:, i * COLS:i * COLS + c1 - c0], [cores[r]],
                      [T.land[:, s * COLS + c0:s * COLS + c1]], T.sem["d%d" % s], topo.mask(core, cores[r]))
    g.wait_ge(T.sem.snt, sent)


def rank_program(g, core, T, topo):
    cores, near_out, near_in, far, fwd, route, tasks, lmask = _plan(T, topo)
    rank = T.rank_of(core)
    if rank is None:
        if core in tasks:
            _helper(g, core, T, topo, cores, tasks[core], lmask)
        return
    s = rank
    sem = T.sem
    v, a, pe, sy = g.vector, g.scalar, g.tensor, g.sync

    for q in range(8):
        (sy if q % 2 == 0 else a).dma_start(T.rep[16 * q:16 * q + 16, :], T.idx[:, :]).then_inc(sem.rep, 16)
    sy.dma_start(T.win[:, PAD:PAD + PART], T.tab[:, :]).then_inc(sem.tabl, 16)
    a.dma_start(T.xs[:, :], T.x[:, :]).then_inc(sem.xl, 16)
    a.wait_ge(sem.rep, 128)
    a.dma_start(T.lists[:, s * K:(s + 1) * K], T.rep[:, :]).then_inc(sem.ownl, 16)

    v.memset(T.ident[:, :], 1.0).then_inc(sem.one, 1)
    v.memset(T.win[:, 0:PAD], 0.0).then_inc(sem.pad, 1)
    v.memset(T.win[:, PAD + PART:WIN], 0.0).then_inc(sem.pad, 1)
    g.wait_ge(sem.one, 1)
    g.affine_select(T.ident[:, :], T.ident[:, :], [[-1, 128]], AluOpType.is_equal, 0.0, 0, 1).then_inc(sem.idn, 1)

    sent = 0
    helpers = []
    for r in far[s]:
        if fwd[s][r] not in helpers:
            helpers.append(fwd[s][r])
    g.wait_ge(sem.rep, 128)
    sent += _send(g, T, topo, T.rep[:, :], helpers, [T.rep[:, :] for h in helpers], sem.lst, lmask[s])
    to = [cores[r] for r in near_out[s]]
    sent += _send(g, T, topo, T.rep[:, :], to, [T.lists[:, s * K:(s + 1) * K] for c in to], sem["l%d" % s],
                  _common(topo, core, to))

    for q in (v, a):
        q.wait_ge(sem.pad, 2)
        q.wait_ge(sem.tabl, 16)

    def offsets(r):
        if r == s:
            v.wait_ge(sem.ownl, 16)
        else:
            v.wait_ge(sem["l%d" % r], _bits(topo.mask(fwd[r][s] if s in fwd[r] else cores[r], core)))
        v.tensor_scalar(T.off[:, r * K:(r + 1) * K], T.lists[:, r * K:(r + 1) * K], PAD - PART * s, PAD + PART,
                        AluOpType.add, AluOpType.min).then_inc(sem["o%d" % r], 1)

    def gather(r):
        v.wait_ge(sem["o%d" % r], 1)
        a.wait_ge(sem["o%d" % r], 1)
        a.activation(T.blk[:, r * COLS:r * COLS + SP], T.win[:, 0:WIN].indirect(T.off[:, r * K:r * K + KS]),
                     ActivationFunctionType.Copy).then_inc(sem["gs%d" % r], 1)
        v.tensor_copy(T.blk[:, r * COLS + SP:(r + 1) * COLS],
                      T.win[:, 0:WIN].indirect(T.off[:, r * K + KS:(r + 1) * K])).then_inc(sem["gv%d" % r], 1)

    hold = 1 if len(near_in[s]) >= 4 else 0
    first = near_in[s][:len(near_in[s]) - hold]
    last = near_in[s][len(near_in[s]) - hold:]
    ahead = len(far[s]) > 2
    for r in [s] + first:
        offsets(r)
        gather(r)
    if ahead:
        offsets(far[s][0])
    for i, r in enumerate(far[s]):
        if not ahead:
            offsets(r)
        elif i + 1 < len(far[s]):
            offsets(far[s][i + 1])
        gather(r)
    for r in last:
        offsets(r)
        gather(r)

    for r in first + far[s] + last:
        if r in route[s]:
            for h, i, c0, c1, mask in route[s][r]:
                if c0 < SP:
                    g.wait_ge(sem["gs%d" % r], 1)
                if c1 > SP:
                    g.wait_ge(sem["gv%d" % r], 1)
                sent += _send(g, T, topo, T.blk[:, r * COLS + c0:r * COLS + c1], [h],
                              [T.rly[:, i * COLS:i * COLS + c1 - c0]], sem["h%d" % i], mask)
        else:
            g.wait_ge(sem["gs%d" % r], 1)
            g.wait_ge(sem["gv%d" % r], 1)
            sent += _send(g, T, topo, T.blk[:, r * COLS:(r + 1) * COLS], [cores[r]],
                          [T.land[:, s * COLS:(s + 1) * COLS]], sem["d%d" % s], topo.mask(core, cores[r]))

    pe.wait_ge(sem.idn, 1)
    pe.wait_ge(sem.xl, 16)
    pe.matmul(T.acc[:, :], T.ident[:, :], T.xs[:, :], True, False)
    pe.wait_ge(sem["gs%d" % s], 1)
    pe.wait_ge(sem["gv%d" % s], 1)
    pe.matmul(T.acc[:, :], T.ident[:, :], T.blk[:, s * COLS:(s + 1) * COLS], False, False)
    straight = [o for o in near_out[s] if s not in route[o]]
    passed = [o for o in near_out[s] if s in route[o]]
    late = sorted(far[s], key=lambda o: far[o].index(s))
    order = straight[:len(straight) - hold] + passed + straight[len(straight) - hold:] + late

    def landed(o):
        if s in route[o]:
            return sum(_bits(topo.mask(p[0], core)) for p in route[o][s])
        return _bits(topo.mask(cores[o], core))

    for n_, o in enumerate(order[:-1]):
        pe.wait_ge(sem["d%d" % o], landed(o))
        mm = pe.matmul(T.acc[:, :], T.ident[:, :], T.land[:, o * COLS:(o + 1) * COLS], False, n_ == len(order) - 2)
        if n_ == len(order) - 2:
            mm.then_inc(sem.pe, 1)
    o = order[-1]
    v.wait_ge(sem.pe, 1)
    v.wait_ge(sem["d%d" % o], landed(o))
    v.tensor_tensor(T.res[:, :], T.acc[:, :], T.land[:, o * COLS:(o + 1) * COLS], AluOpType.add).then_inc(sem.cp, 1)
    sy.wait_ge(sem.cp, 1)
    sy.dma_start(T.y[:, :], T.res[:, :]).then_inc(sem.st, 16)
    sy.wait_ge(sem.st, 16)
    g.wait_ge(sem.snt, sent)
